import numpy as np, ml_dtypes
CORES = [29,45,93,109,157,173,221,237,285,301,349,365,413,429,477,493]
N = 16
NP, NBK, TK, CAP = 8, 4, 128, 7
DEST = [[11,14,11,8],[14,12,8,8],[14,15,12,15],[8,12,11,10],[14,9,13,14],[10,13,13,11],[10,10,10,13],[13,10,11,10]]
def setup_inputs(rng):
    return {"x": rng.standard_normal((N, 128, NBK * TK), dtype=np.float32).astype(ml_dtypes.bfloat16), "w": (rng.standard_normal((N, 128, 128), dtype=np.float32) / 8).astype(ml_dtypes.bfloat16)}
def setup_inputs_big(rng):
    d = setup_inputs(rng)
    for k in ("x", "w"): d[k] = (d[k].astype(np.float32) * 1024.0).astype(d[k].dtype)
    return d
def setup_inputs_small(rng):
    d = setup_inputs(rng)
    for k in ("x", "w"): d[k] = (d[k].astype(np.float32) * (1 / 1024.0)).astype(d[k].dtype)
    return d
def reference(x, w):
    X, W = x.astype(np.float64), w.astype(np.float64)
    y = np.full((N, 128, CAP * TK), np.nan); n = [0] * N
    for p in range(NP):
        for c in range(NBK):
            q = DEST[p][c]
            y[q][:, TK * n[q]:TK * n[q] + TK] = W[q].T @ np.maximum(W[p].T @ X[p][:, TK * c:TK * c + TK], 0.0)
            n[q] += 1
    return {"y": y.astype(ml_dtypes.bfloat16 if x.dtype != np.float64 else np.float64)}

from concourse.mybir import AluOpType

TK = 128
NBK = 4
CAP = 7
NPIECE = 8
FWD_CAP = 3

SCRATCH = {
    "wb": ("sbuf", [128, TK], "bfloat16"),
    "xb": ("sbuf", [128, NBK * TK], "bfloat16"),
    "zero": ("sbuf", [128, NBK * TK], "bfloat16"),
    "hb": ("sbuf", [128, NBK * TK], "bfloat16"),
    "land": ("sbuf", [128, CAP * TK], "bfloat16"),
    "ob": ("sbuf", [128, CAP * TK], "bfloat16"),
}
for _i in range(NPIECE):
    SCRATCH["ps%d" % _i] = ("psum", [128, 512], "float32")

SEMAPHORES = ["wl", "xl", "zs", "sent", "st"] + ["%s%d" % (n, i) for n in ("mm", "ev", "arr") for i in range(NPIECE)]


def _plan(T, topo):
    cores, dest = T.cores, T.tables["DEST"]
    n_p = len(dest)
    nslot, groups = {}, []
    for p in range(n_p):
        byq = {}
        for c, q in enumerate(dest[p]):
            s = nslot.get(q, 0)
            nslot[q] = s + 1
            if q not in byq:
                byq[q] = {"p": p, "q": q, "cs": [], "s0": s, "via": None}
                groups.append(byq[q])
            byq[q]["cs"].append(c)
    for gr in groups:
        gr["k"] = len(gr["cs"])

    def can_pass(r, gr):
        return (r != gr["p"] and topo.same_plane(cores[gr["p"]], cores[r]) and topo.may_write(cores[gr["p"]], cores[r])
                and topo.may_write(cores[r], cores[gr["q"]]))

    writes = [sum(1 for gr in groups if gr["p"] == p) for p in range(n_p)]
    held = {}
    spill = {}
    for gr in groups:
        if topo.may_write(cores[gr["p"]], cores[gr["q"]]):
            continue
        near = [r for r in range(n_p) if can_pass(r, gr) and topo.chip(cores[r]) == topo.chip(cores[gr["q"]])]
        if near and held.get((near[0], gr["q"]), 0) + gr["k"] <= FWD_CAP:
            r = near[0]
            if (r, gr["q"]) not in held:
                writes[r] += 1
            held[(r, gr["q"])] = held.get((r, gr["q"]), 0) + gr["k"]
            gr["via"] = r
        else:
            spill.setdefault(gr["q"], []).append(gr)
    for q in sorted(spill):
        senders = set(gr["p"] for gr in spill[q])
        cand = [r for r in range(n_p) if all(can_pass(r, gr) for gr in spill[q]) and (r, q) not in held]
        shared = dict((r, all(any(o["p"] == p and o["via"] == r for o in groups) for p in senders)) for r in cand)
        r = min(cand, key=lambda r: (not shared[r], writes[r], r))
        writes[r] += 1
        for gr in spill[q]:
            gr["via"] = r
        if shared[r]:
            for p in senders:
                writes[p] -= 1

    fwds = []
    for gr in sorted((gr for gr in groups if gr["via"] is not None), key=lambda gr: (gr["via"], gr["q"], gr["s0"])):
        f = fwds[-1] if fwds else None
        if f and f["r"] == gr["via"] and f["q"] == gr["q"] and f["s0"] + f["k"] == gr["s0"]:
            f["parts"].append(gr)
            f["k"] += gr["k"]
        else:
            f = {"r": gr["via"], "q": gr["q"], "s0": gr["s0"], "k": gr["k"], "parts": [gr]}
            fwds.append(f)
        gr["fwd"] = f
    passes = []
    for r in range(n_p):
        mine = sorted((f for f in fwds if f["r"] == r), key=lambda f: (-f["k"], f["q"]))
        col = 0
        for i, f in enumerate(mine):
            f["turn"] = i
            for gr in f["parts"]:
                gr["col"] = col
                col += gr["k"]
        passes.append(mine)

    sends = []
    for p in range(n_p):
        mine = []
        for gr in sorted((gr for gr in groups if gr["p"] == p and gr["via"] is not None), key=lambda gr: (gr["via"], gr["col"])):
            b = mine[-1] if mine else None
            if b and b["to"] == gr["via"] and b["col"] + b["k"] == gr["col"]:
                b["groups"].append(gr)
                b["k"] += gr["k"]
            else:
                mine.append({"p": p, "to": gr["via"], "col": gr["col"], "k": gr["k"], "groups": [gr]})
        for b in mine:
            b["key"] = (0, -len(set(gr["q"] for gr in b["groups"])), -max(gr["fwd"]["k"] for gr in b["groups"]), -b["k"], b["to"])
        for gr in groups:
            if gr["p"] == p and gr["via"] is None:
                mine.append({"p": p, "to": gr["q"], "col": gr["s0"], "k": gr["k"], "groups": [gr],
                             "key": (1, -nslot[gr["q"]], -gr["k"], gr["q"])})
        mine.sort(key=lambda b: b["key"])
        for i, b in enumerate(mine):
            b["turn"] = i
            for gr in b["groups"]:
                gr["bundle"] = b
        sends.append(mine)

    lands = {}
    for f in fwds:
        f["when"] = (1, max(gr["bundle"]["turn"] for gr in f["parts"]) + f["turn"], f["s0"])
    for rank in range(len(cores)):
        a = [b for mine in sends for b in mine if b["to"] == rank]
        for b in a:
            b["when"] = (0, b["turn"], b["col"])
        a += [f for f in fwds if f["q"] == rank]
        a.sort(key=lambda e: e["when"])
        for j, e in enumerate(a):
            e["sem"] = j
        lands[rank] = a
    return sends, passes, lands


def _engines(topo, src, dst):
    return bin(topo.mask(src, dst)).count("1")


def _write(g, T, topo, src, dst, out_ap, in_ap, sem):
    rid, pid = topo.addr(dst, src)
    g.remote_dma(out_ap=out_ap, in_ap=in_ap, remote_sem=sem, local_sem=T.sem.sent, pid=pid, routing_id=rid,
                 dma_engine_mask=topo.mask(src, dst))
    return _engines(topo, src, dst)


def rank_program(g, core, T, topo):
    rank = T.rank_of(core)
    if rank is None:
        return
    cores, S = T.cores, T.sem
    sends, passes, lands = _plan(T, topo)

    g.scalar.dma_start(T.wb[:], T.w[:]).then_inc(S.wl, 16)

    if rank < len(sends):
        g.sync.dma_start(T.xb[:], T.x[:]).then_inc(S.xl, 16)
        g.vector.memset(T.zero[:], 0.0).then_inc(S.zs, 1)
        g.vector.wait_ge(S.zs, 1)
        g.tensor.wait_ge(S.wl, 16)
        g.tensor.wait_ge(S.xl, 16)
        left, col = 0, 0
        for i, b in enumerate(sends[rank]):
            ps, wd = T["ps%d" % i], b["k"] * TK
            runs = []
            for c in [c for gr in b["groups"] for c in gr["cs"]]:
                if runs and runs[-1][0] + runs[-1][1] == c:
                    runs[-1][1] += 1
                else:
                    runs.append([c, 1])
            j = 0
            for c0, n in runs:
                g.tensor.matmul(ps[:, j * TK:(j + n) * TK], T.wb[:], T.xb[:, c0 * TK:(c0 + n) * TK],
                                start=True, stop=True).then_inc(S["mm%d" % i], 1)
                j += n
            g.vector.wait_ge(S["mm%d" % i], len(runs))
            g.vector.tensor_tensor(T.hb[:, col:col + wd], ps[:, 0:wd], T.zero[:, 0:wd], AluOpType.max).then_inc(S["ev%d" % i], 1)
            g.wait_ge(S["ev%d" % i], 1)
            left += _write(g, T, topo, core, cores[b["to"]], T.land[:, b["col"] * TK:b["col"] * TK + wd],
                           T.hb[:, col:col + wd], S["arr%d" % b["sem"]])
            col += wd
        seen = set()
        for f in passes[rank]:
            for gr in f["parts"]:
                b = gr["bundle"]
                if b["sem"] not in seen:
                    seen.add(b["sem"])
                    g.wait_ge(S["arr%d" % b["sem"]], _engines(topo, cores[b["p"]], core))
            at = f["parts"][0]["col"]
            left += _write(g, T, topo, core, cores[f["q"]], T.land[:, f["s0"] * TK:(f["s0"] + f["k"]) * TK],
                           T.land[:, at * TK:(at + f["k"]) * TK], S["arr%d" % f["sem"]])
        g.wait_ge(S.sent, left)
        return

    g.tensor.wait_ge(S.wl, 16)
    mine = lands[rank]
    for j, a in enumerate(mine):
        src = cores[a["r"]] if "r" in a else cores[a["p"]]
        s0 = a["s0"] if "r" in a else a["col"]
        ps, lo, wd = T["ps%d" % j], s0 * TK, a["k"] * TK
        g.tensor.wait_ge(S["arr%d" % j], _engines(topo, src, core))
        g.tensor.matmul(ps[:, 0:wd], T.wb[:], T.land[:, lo:lo + wd], start=True, stop=True).then_inc(S["mm%d" % j], 1)
        g.vector.wait_ge(S["mm%d" % j], 1)
        g.vector.tensor_copy(T.ob[:, lo:lo + wd], ps[:, 0:wd]).then_inc(S["ev%d" % j], 1)
        dq = g.sync if j % 2 == 0 else g.scalar
        dq.wait_ge(S["ev%d" % j], 1)
        dq.dma_start(T.y[:, lo:lo + wd], T.ob[:, lo:lo + wd]).then_inc(S.st, 16)
    g.wait_ge(S.st, 16 * len(mine))
